import numpy as np
import ml_dtypes


def mxq(x, axis, fmt="e4m3"):
    dtype, down = {"e4m3": (ml_dtypes.float8_e4m3fn, 7), "e5m2": (ml_dtypes.float8_e5m2, 14)}[fmt]
    v = np.moveaxis(np.asarray(x, np.float32).astype(ml_dtypes.bfloat16).astype(np.float64), axis, -1)
    blocks = v.reshape(v.shape[:-1] + (-1, 32))
    amax = np.abs(blocks).max(-1, keepdims=True)
    byte = np.maximum(np.where(amax > 0, np.frexp(amax)[1] - 1 + 127, 0) - down, 1)
    scale = np.exp2(byte - 127.0)
    codes = (blocks / scale).astype(np.float32).astype(dtype).astype(np.float64)
    return np.moveaxis((codes * scale).reshape(v.shape), -1, axis)


WIDE = False


def mx_kscale(k):
    if not WIDE:
        return np.ones(k)
    levels = np.array([30, -30])
    if k % 512:
        return np.exp2(np.random.permutation(np.resize(levels, k // 32))).repeat(32)
    a = np.empty((k // 512, 16))
    for p in range(k // 512):
        a[p, :8] = np.random.permutation(np.resize(levels, 8))
        for g in range(8):
            far = levels[np.abs(levels - a[p, g]) >= 10]
            a[p, g + 8] = far[np.random.randint(len(far))]
    return np.exp2(a.ravel()).repeat(32)


def f64(x):
    return np.asarray(x).astype(np.float64)


def striped(idx):
    return np.tile(np.asarray(idx).reshape(-1, 16).T, (8, 1)).astype(np.uint16)


def unstriped(offs):
    return offs[:16].T.reshape(-1).astype(np.int64)


E2M1 = np.array([0.0, 0.5, 1.0, 1.5, 2.0, 3.0, 4.0, 6.0, -0.0, -0.5, -1.0, -1.5, -2.0, -3.0, -4.0, -6.0])


def pack_weight(w, fmt):
    k, n = w.shape
    w = f64(np.asarray(w, np.float32).astype(ml_dtypes.bfloat16)).reshape(k // 32, 32, n)
    amax = np.abs(w).max(1)
    if fmt in ("e4m3", "e5m2"):
        byte = np.frexp(amax)[1] - 1 + 127 - (7 if fmt == "e4m3" else 14)
    else:
        mant, ex = np.frexp(amax / 6.0)
        byte = np.where(mant > 0.5, ex, ex - 1) + 127
    byte = np.clip(np.where(amax > 0, byte, 1), 1, 254)
    scaled = (w * np.exp2(127.0 - byte)[:, None, :]).reshape(k, n).astype(np.float32)
    by_word = np.ascontiguousarray(scaled.reshape(k // 512, 128, 4, n).transpose(0, 1, 3, 2))
    if fmt in ("e4m3", "e5m2"):
        words = by_word.astype(ml_dtypes.float8_e4m3fn if fmt == "e4m3" else ml_dtypes.float8_e5m2).view(np.uint8)
    else:
        c = by_word.astype(ml_dtypes.float4_e2m1fn).view(np.uint8) & 0xF
        words = (c[..., 0::2] | (c[..., 1::2] << 4)).reshape(k // 512, 128, 2 * n)
    return np.ascontiguousarray(words), np.ascontiguousarray(byte.astype(np.uint8).reshape(k // 512, 16, n))


def unpack_weight(words, scales, fmt):
    g, _, n = scales.shape
    words = np.ascontiguousarray(words).reshape(g, 128, n, -1)
    if fmt in ("e4m3", "e5m2"):
        vals = words.view(ml_dtypes.float8_e4m3fn if fmt == "e4m3" else ml_dtypes.float8_e5m2).astype(np.float64)
    else:
        nib = np.empty((g, 128, n, 4), np.uint8)
        nib[..., 0::2] = words & 0xF
        nib[..., 1::2] = words >> 4
        vals = E2M1[nib]
    vals = vals * np.repeat(np.exp2(scales.astype(np.float64) - 127.0), 8, axis=1)[..., None]
    return vals.transpose(0, 1, 3, 2).reshape(g * 512, n)


def sigmoid(v):
    return 1.0 / (1.0 + np.exp(-v))


def sgn(shape):
    return np.random.uniform(0.5, 2.0, shape) * np.where(np.random.standard_normal(shape) < 0, -1.0, 1.0)


K, T, J, R, V, N, U, E = 512, 1024, 256, 512, 1024, 256, 128, 512


def setup_inputs():
    n = np.random.standard_normal
    idx = np.random.permutation(V)[:R]
    idx2 = np.random.permutation(T)[:J]
    idx3 = np.random.permutation(J)[:U]
    idx4 = np.random.permutation(J)[:U]
    idx5 = np.random.permutation(E)[:U]
    idx6 = np.random.permutation(E)[:J]
    fk = mx_kscale(K)
    fr = mx_kscale(R)
    tr = np.ones(V)
    tr[idx] = fr
    xtp = pack_weight(n((K, T)) / fk[:, None], "e5m2")
    wtp = pack_weight(n((K, V)) * 1 / np.sqrt(K) * fk[:, None] * tr, "e2m1")
    w2p = pack_weight(n((K, R)) * 1 / np.sqrt(K) * fk[:, None] * fr, "e4m3")
    wbp = pack_weight(n((R, N)) * 1 / np.sqrt(R) / fr[:, None], "e2m1")
    wcp = pack_weight(n((R, N)) * 1 / np.sqrt(R) / fr[:, None], "e4m3")
    return {
        "xt_words": xtp[0],
        "xt_scales": xtp[1],
        "wt_words": wtp[0],
        "wt_scales": wtp[1],
        "w2_words": w2p[0],
        "w2_scales": w2p[1],
        "wb_words": wbp[0],
        "wb_scales": wbp[1],
        "wc_words": wcp[0],
        "wc_scales": wcp[1],
        "so": (np.random.uniform(0.5, 1.6, (N, 1))).astype(np.float32),
        "sp": (sgn((N, 1))).astype(np.float32),
        "bo": (np.random.uniform(-2.0, 2.0, (N, 1))).astype(np.float32),
        "offs": striped(idx),
        "offs2": striped(idx2),
        "offs3": striped(idx3),
        "offs4": striped(idx4),
        "offs5": striped(idx5),
        "offs6": striped(idx6),
    }


def reference(xt_words, xt_scales, wt_words, wt_scales, w2_words, w2_scales, wb_words, wb_scales, wc_words, wc_scales, so, sp, bo, offs, offs2, offs3, offs4, offs5, offs6):
    idx = unstriped(offs)
    idx2 = unstriped(offs2)
    idx3 = unstriped(offs3)
    idx4 = unstriped(offs4)
    idx5 = unstriped(offs5)
    idx6 = unstriped(offs6)
    xtu = unpack_weight(xt_words, xt_scales, "e5m2")
    wtu = unpack_weight(wt_words, wt_scales, "e2m1")
    w2u = unpack_weight(w2_words, w2_scales, "e4m3")
    wbu = unpack_weight(wb_words, wb_scales, "e2m1")
    wcu = unpack_weight(wc_words, wc_scales, "e4m3")
    wtidxg = wtu[:, idx]
    xtidx2g = xtu[:, idx2]
    a = wtidxg.T @ xtidx2g
    b = w2u.T @ xtidx2g
    hid = np.abs(a - b)
    hidq = mxq(hid, 0, "e4m3")
    p = wbu.T @ hidq
    q = wcu.T @ hidq
    m0 = p[:, idx3] * f64(so) * sigmoid(p[:, idx4] * f64(sp) + f64(bo))
    pw = np.zeros((N, E))
    pw[:, idx5] = m0
    pv = np.zeros((N, E))
    pv[:, idx6] = q
    y = pw + pv
    return y

@@ -1,0 +1,244 @@
+from contextlib import ExitStack
+
+import concourse.mybir as mybir
+from concourse.masks import make_identity
+
+K, T, J, R, V, N, U, E = 512, 1024, 256, 512, 1024, 256, 128, 512
+FLOPS = 2 * K * R * J * 2 + 2 * R * N * J * 2
+
+F32 = mybir.dt.float32
+BF16 = mybir.dt.bfloat16
+I32 = mybir.dt.int32
+U32 = mybir.dt.uint32
+U16 = mybir.dt.uint16
+U8 = mybir.dt.uint8
+E4M3 = mybir.dt.float8_e4m3fn_x4
+E5M2 = mybir.dt.float8_e5m2_x4
+E2M1 = mybir.dt.float4_e2m1fn_x4
+ACT = mybir.ActivationFunctionType
+ALU = mybir.AluOpType
+
+P = 128
+PACK = 4
+LIST_COL = 16
+R_HEAD = 384
+
+
+def tile_list_outcomegatedpages_storeleads_kernel(
+    tc, xt_words, xt_scales, wt_words, wt_scales, w2_words, w2_scales, wb_words, wb_scales,
+    wc_words, wc_scales, so, sp, bo, offs, offs2, offs3, offs4, offs5, offs6, out,
+):
+    nc = tc.nc
+    with ExitStack() as ctx:
+        sb = ctx.enter_context(tc.tile_pool(name="sb", bufs=1))
+        ps = ctx.enter_context(tc.psum_pool(name="ps", bufs=1))
+
+        def sbuf(name, shape, dtype):
+            return sb.tile(shape, dtype, name=name, align_bytes=64)
+
+        def bank(name, shape, tag):
+            return ps.tile(shape, F32, name=name, tag=tag)
+
+        def load_list(name, source):
+            held = sbuf(name, list(source.shape), U16)
+            nc.sync.dma_start(held[:], source)
+            return held
+
+        def load_words(name, source, width, dtype):
+            held = sbuf(name, [P, width], dtype)
+            nc.sync.dma_start(held[:].bitcast(I32), source.bitcast(I32))
+            return held
+
+        def zeroed_scales(name, width):
+            held = sbuf(name, [P, width], U8)
+            nc.vector.memset(held[:].bitcast(I32), 0)
+            return held
+
+        def load_scale_rows(queue, held, source, quadrants):
+            for quadrant in quadrants:
+                queue.dma_start(
+                    held[32 * quadrant : 32 * quadrant + 4, :].bitcast(I32),
+                    source[0, 4 * quadrant : 4 * quadrant + 4, :].bitcast(I32),
+                )
+
+        def fp8_words(source):
+            return source[0].rearrange("p c r -> p (c r)")
+
+        def load_column_pair(name, source):
+            held = sbuf(name, [P, N // P], F32)
+            with nc.allow_non_contiguous_dma(reason="one value a partition for each tile of n"):
+                nc.sync.dma_start(held[:], source.rearrange("(t p) o -> p (t o)", p=P))
+            return held
+
+        xs_all = zeroed_scales("xs_all", T)
+        w2s = zeroed_scales("w2s", R)
+        ws_all = zeroed_scales("ws_all", V)
+        wcs = zeroed_scales("wcs", N)
+        wbs = zeroed_scales("wbs", N)
+
+        ww_all = load_words("ww_all", wt_words[0], V, U16)
+        idx = load_list("idx", offs)
+        idx2 = load_list("idx2", offs2)
+        load_scale_rows(nc.sync, xs_all, xt_scales, (0, 1, 2))
+        load_scale_rows(nc.gpsimd, xs_all, xt_scales, (3,))
+        xw_all = load_words("xw_all", fp8_words(xt_words), T, U32)
+        w2w = load_words("w2w", fp8_words(w2_words), R, U32)
+        load_scale_rows(nc.sync, w2s, w2_scales, (0, 1))
+        load_scale_rows(nc.gpsimd, w2s, w2_scales, (2, 3))
+        load_scale_rows(nc.sync, ws_all, wt_scales, range(4))
+        wcw = load_words("wcw", fp8_words(wc_words), N, U32)
+        load_scale_rows(nc.sync, wcs, wc_scales, range(4))
+        idx6 = load_list("idx6", offs6)
+        idx4 = load_list("idx4", offs4)
+        idx3 = load_list("idx3", offs3)
+        sp_col = load_column_pair("sp_col", sp)
+        bo_col = load_column_pair("bo_col", bo)
+        so_col = load_column_pair("so_col", so)
+        idx5 = load_list("idx5", offs5)
+        wbw = load_words("wbw", wb_words[0], N, U16)
+        load_scale_rows(nc.sync, wbs, wb_scales, range(4))
+
+        identity = sbuf("identity", [P, P], F32)
+        make_identity(nc, identity[:])
+
+        pw = [sbuf(f"pw{n}", [P, E], F32) for n in range(N // P)]
+        pv = [sbuf(f"pv{n}", [P, E], F32) for n in range(N // P)]
+        for page in pv:
+            nc.vector.memset(page[:], 0.0)
+        for page in pw:
+            nc.gpsimd.memset(page[:], 0.0)
+
+        xw = sbuf("xw", [P, J], U32)
+        xs = sbuf("xs", [P, J], U8)
+        ww = sbuf("ww", [P, R], U16)
+        ws = sbuf("ws", [P, R], U8)
+
+        def gather(picked, table, listed, first, last):
+            nc.vector.tensor_copy(
+                picked[:, first:last], table[:].indirect(listed[:, first // LIST_COL : last // LIST_COL])
+            )
+
+        def first_product(acc, jt, words, scales, dtype, first, last):
+            cols = slice(jt * P, (jt + 1) * P)
+            nc.tensor.matmul_mx(
+                acc, lhsT=xw[:, cols].bitcast(E5M2), lhsT_scale=xs[:, cols],
+                rhs=words[:, first:last].bitcast(dtype), rhs_scale=scales[:, first:last],
+                start=True, stop=True,
+            )
+
+        def by_slot(ap):
+            return ap.rearrange("p (m t) -> p t m", t=PACK)
+
+        gather(ww, ww_all, idx, 0, R_HEAD)
+        gather(xw, xw_all, idx2, 0, J)
+        gather(xs, xs_all, idx2, 0, J)
+
+        b_sb = []
+        for jt in range(J // P):
+            b_ps = bank(f"b_ps{jt}", [P, R], f"turn{jt}")
+            first_product(b_ps[:], jt, w2w, w2s, E4M3, 0, R)
+            held = sbuf(f"b_sb{jt}", [P, PACK, R // PACK], F32)
+            nc.scalar.copy(held[:], by_slot(b_ps[:]))
+            b_sb.append(held)
+
+        gather(ws, ws_all, idx, 0, R_HEAD)
+        a0_head = bank("a0_head", [P, R_HEAD], "a0_head")
+        first_product(a0_head[:, 0:256], 0, ww, ws, E2M1, 0, 256)
+        first_product(a0_head[:, 256:R_HEAD], 0, ww, ws, E2M1, 256, R_HEAD)
+        gather(ww, ww_all, idx, R_HEAD, R)
+        gather(ws, ws_all, idx, R_HEAD, R)
+        a0_tail = bank("a0_tail", [P, R - R_HEAD], "a0_tail")
+        first_product(a0_tail[:], 0, ww, ws, E2M1, R_HEAD, R)
+        a1 = bank("a1", [P, R], "a1")
+        first_product(a1[:], 1, ww, ws, E2M1, 0, R)
+
+        diff = [sbuf(f"diff{jt}", [P, PACK, R // PACK], F32) for jt in range(J // P)]
+
+        def subtract(jt, acc, first, last):
+            part = slice(first // PACK, last // PACK)
+            nc.vector.tensor_tensor(diff[jt][:, :, part], by_slot(acc), b_sb[jt][:, :, part], ALU.subtract)
+
+        subtract(0, a0_head[:], 0, R_HEAD)
+        subtract(0, a0_tail[:], R_HEAD, R)
+        subtract(1, a1[:], 0, R)
+
+        hid_bf = []
+        for jt in range(J // P):
+            turned = bank(f"turned{jt}", [P, PACK, P], f"turn{jt}")
+            for t in range(PACK):
+                nc.tensor.transpose(turned[:, t, :], diff[jt][:, t, :], identity[:])
+            held = sbuf(f"hid_bf{jt}", [P, P, PACK], BF16)
+            nc.scalar.activation(held[:], turned[:].rearrange("p t j -> p j t"), ACT.Abs)
+            hid_bf.append(held)
+
+        codes = sbuf("hid_codes", [P, J], U32)
+        scales = sbuf("hid_scales", [P, J], U8)
+        for jt in range(J // P):
+            cols = slice(jt * P, (jt + 1) * P)
+            nc.vector.quantize_mx(
+                codes[:, cols].bitcast(E4M3), scales[:, cols], hid_bf[jt][:].rearrange("p j t -> p (j t)")
+            )
+
+        def second_product(acc, words, wscales, dtype, n, first, last):
+            cols = slice(n * P, (n + 1) * P)
+            nc.tensor.matmul_mx(
+                acc, lhsT=words[:, cols].bitcast(dtype), lhsT_scale=wscales[:, cols],
+                rhs=codes[:, first:last].bitcast(E4M3), rhs_scale=scales[:, first:last], start=True, stop=True,
+            )
+
+        q_sb = sbuf("q_sb", [P, N // P, J], F32)
+
+        def q_window(n, first, last):
+            return pv[n][:].indirect(idx6[:, first // LIST_COL : last // LIST_COL])
+
+        def put_q_vector(n, first, last):
+            nc.vector.tensor_copy(q_window(n, first, last), q_sb[:, n, first:last])
+
+        def put_q_scalar(n, first, last):
+            nc.scalar.activation(q_window(n, first, last), q_sb[:, n, first:last], ACT.Copy)
+
+        def look(n, p_sb):
+            gate = sbuf(f"gate{n}", [P, U], F32)
+            nc.scalar.activation(
+                gate[:], p_sb[:].indirect(idx4[:]), ACT.Sigmoid,
+                bias=bo_col[:, n : n + 1], scale=sp_col[:, n : n + 1],
+            )
+            weighted = sbuf(f"weighted{n}", [P, U], F32)
+            nc.scalar.activation(weighted[:], p_sb[:].indirect(idx3[:]), ACT.Copy, scale=so_col[:, n : n + 1])
+            return weighted, gate
+
+        def put_m0(n, weighted, gate):
+            nc.vector.tensor_tensor(pw[n][:].indirect(idx5[:]), weighted[:], gate[:], ALU.mult)
+
+        def add_and_store(n):
+            result = sbuf(f"result{n}", [P, E], F32)
+            nc.vector.tensor_tensor(result[:], pw[n][:], pv[n][:], ALU.add)
+            nc.sync.dma_start(out[n * P : (n + 1) * P, :], result[:])
+
+        p_sb = [sbuf(f"p_sb{n}", [P, J], F32) for n in range(N // P)]
+
+        q0_ps = [bank("q_ps00", [P, P], "q0"), bank("q_ps01", [P, P], "a0_tail")]
+        for n in range(N // P):
+            second_product(q0_ps[n][:], wcw, wcs, E4M3, n, 0, P)
+        nc.scalar.copy(q_sb[:, 0, 0:P], q0_ps[0][:])
+        put_q_scalar(0, 0, P)
+        nc.vector.tensor_copy(q_sb[:, 1, 0:P], q0_ps[1][:])
+
+        p_ps = [bank(f"p_ps{n}", [P, J], f"p{n}") for n in range(N // P)]
+        for n in range(N // P):
+            second_product(p_ps[n][:], wbw, wbs, E2M1, n, 0, J)
+        for n in range(N // P):
+            nc.vector.tensor_copy(p_sb[n][:], p_ps[n][:])
+        q1_ps = bank("q_ps1", [P, N // P, P], "p0")
+        for n in range(N // P):
+            second_product(q1_ps[:, n, :], wcw, wcs, E4M3, n, P, J)
+        nc.vector.tensor_copy(q_sb[:, :, P:J], q1_ps[:])
+        looks0 = look(0, p_sb[0])
+        looks1 = look(1, p_sb[1])
+        put_q_vector(0, P, P + 64)
+        put_q_scalar(0, P + 64, J)
+        put_q_scalar(1, 0, J)
+        put_m0(0, *looks0)
+        put_m0(1, *looks1)
+        add_and_store(0)
+        add_and_store(1)

@@ -44,21 +44,21 @@ def tile_list_outcomegatedpages_storeleads_kernel(
             nc.sync.dma_start(held[:], source)
             return held
 
-        def load_words(name, source, width, dtype):
+        def load_words(name, source, width, dtype, queue):
             held = sbuf(name, [P, width], dtype)
-            nc.sync.dma_start(held[:].bitcast(I32), source.bitcast(I32))
+            queue.dma_start(held[:].bitcast(I32), source.bitcast(I32))
             return held
 
-        def zeroed_scales(name, width):
+        def zeroed_scales(name, width, engine):
             held = sbuf(name, [P, width], U8)
-            nc.vector.memset(held[:].bitcast(I32), 0)
+            engine.memset(held[:].bitcast(I32), 0)
             return held
 
         def load_scale_rows(queue, held, source, quadrants):
             for quadrant in quadrants:
                 queue.dma_start(
-                    held[32 * quadrant : 32 * quadrant + 4, :].bitcast(I32),
-                    source[0, 4 * quadrant : 4 * quadrant + 4, :].bitcast(I32),
+                    held[32 * quadrant : 32 * quadrant + 32, :].bitcast(I32),
+                    source[0, 4 * quadrant : 4 * quadrant + 4, :].bitcast(I32).partition_broadcast(8),
                 )
 
         def fp8_words(source):
@@ -70,24 +70,36 @@ def tile_list_outcomegatedpages_storeleads_kernel(
                 nc.sync.dma_start(held[:], source.rearrange("(t p) o -> p (t o)", p=P))
             return held
 
-        xs_all = zeroed_scales("xs_all", T)
-        w2s = zeroed_scales("w2s", R)
-        ws_all = zeroed_scales("ws_all", V)
-        wcs = zeroed_scales("wcs", N)
-        wbs = zeroed_scales("wbs", N)
+        def load_live_rows(held, source):
+            for quadrant in range(4):
+                nc.sync.dma_start(
+                    held[32 * quadrant : 32 * quadrant + 4, :].bitcast(I32),
+                    source[0, 4 * quadrant : 4 * quadrant + 4, :].bitcast(I32),
+                )
 
-        ww_all = load_words("ww_all", wt_words[0], V, U16)
+        wcs = zeroed_scales("wcs", N, nc.vector)
+        wbs = zeroed_scales("wbs", N, nc.vector)
+        xs_all = sbuf("xs_all", [P, T], U8)
+        ws_all = sbuf("ws_all", [P, V], U8)
+        w2s = sbuf("w2s", [P, R], U8)
+
+        ww_all = load_words("ww_all", wt_words[0], V, U16, nc.sync)
+        load_scale_rows(nc.gpsimd, w2s, w2_scales, (2, 3))
         idx = load_list("idx", offs)
         idx2 = load_list("idx2", offs2)
-        load_scale_rows(nc.sync, xs_all, xt_scales, (0, 1, 2))
-        load_scale_rows(nc.gpsimd, xs_all, xt_scales, (3,))
-        xw_all = load_words("xw_all", fp8_words(xt_words), T, U32)
-        w2w = load_words("w2w", fp8_words(w2_words), R, U32)
+        load_scale_rows(nc.sync, xs_all, xt_scales, range(4))
+        xw_all = load_words("xw_all", fp8_words(xt_words), T, U32, nc.sync)
+
+        w2w = load_words("w2w", fp8_words(w2_words), R, U32, nc.sync)
         load_scale_rows(nc.sync, w2s, w2_scales, (0, 1))
-        load_scale_rows(nc.gpsimd, w2s, w2_scales, (2, 3))
         load_scale_rows(nc.sync, ws_all, wt_scales, range(4))
-        wcw = load_words("wcw", fp8_words(wc_words), N, U32)
-        load_scale_rows(nc.sync, wcs, wc_scales, range(4))
+
+        warm_in = sbuf("warm_in", [P, 1], F32)
+        warm_out = sbuf("warm_out", [P, 1], F32)
+        nc.vector.memset(warm_in[:], 0.0)
+        nc.scalar.activation(warm_out[:], warm_in[:], ACT.Sigmoid)
+
+        wcw = load_words("wcw", fp8_words(wc_words), N, U32, nc.sync)
         idx6 = load_list("idx6", offs6)
         idx4 = load_list("idx4", offs4)
         idx3 = load_list("idx3", offs3)
@@ -95,8 +107,9 @@ def tile_list_outcomegatedpages_storeleads_kernel(
         bo_col = load_column_pair("bo_col", bo)
         so_col = load_column_pair("so_col", so)
         idx5 = load_list("idx5", offs5)
-        wbw = load_words("wbw", wb_words[0], N, U16)
-        load_scale_rows(nc.sync, wbs, wb_scales, range(4))
+        wbw = load_words("wbw", wb_words[0], N, U16, nc.sync)
+        load_live_rows(wcs, wc_scales)
+        load_live_rows(wbs, wb_scales)
 
         identity = sbuf("identity", [P, P], F32)
         make_identity(nc, identity[:])
@@ -129,9 +142,9 @@ def tile_list_outcomegatedpages_storeleads_kernel(
         def by_slot(ap):
             return ap.rearrange("p (m t) -> p t m", t=PACK)
 
-        gather(ww, ww_all, idx, 0, R_HEAD)
-        gather(xw, xw_all, idx2, 0, J)
+        gather(ww, ww_all, idx, 0, R)
         gather(xs, xs_all, idx2, 0, J)
+        gather(xw, xw_all, idx2, 0, J)
 
         b_sb = []
         for jt in range(J // P):
@@ -145,7 +158,6 @@ def tile_list_outcomegatedpages_storeleads_kernel(
         a0_head = bank("a0_head", [P, R_HEAD], "a0_head")
         first_product(a0_head[:, 0:256], 0, ww, ws, E2M1, 0, 256)
         first_product(a0_head[:, 256:R_HEAD], 0, ww, ws, E2M1, 256, R_HEAD)
-        gather(ww, ww_all, idx, R_HEAD, R)
         gather(ws, ws_all, idx, R_HEAD, R)
         a0_tail = bank("a0_tail", [P, R - R_HEAD], "a0_tail")
         first_product(a0_tail[:], 0, ww, ws, E2M1, R_HEAD, R)
@@ -210,10 +222,10 @@ def tile_list_outcomegatedpages_storeleads_kernel(
         def put_m0(n, weighted, gate):
             nc.vector.tensor_tensor(pw[n][:].indirect(idx5[:]), weighted[:], gate[:], ALU.mult)
 
-        def add_and_store(n):
-            result = sbuf(f"result{n}", [P, E], F32)
-            nc.vector.tensor_tensor(result[:], pw[n][:], pv[n][:], ALU.add)
-            nc.sync.dma_start(out[n * P : (n + 1) * P, :], result[:])
+        def add_and_store(n, first, last, queue):
+            result = sbuf(f"result{n}_{first}", [P, last - first], F32)
+            nc.vector.tensor_tensor(result[:], pw[n][:, first:last], pv[n][:, first:last], ALU.add)
+            queue.dma_start(out[n * P : (n + 1) * P, first:last], result[:])
 
         p_sb = [sbuf(f"p_sb{n}", [P, J], F32) for n in range(N // P)]
 
@@ -223,6 +235,7 @@ def tile_list_outcomegatedpages_storeleads_kernel(
         nc.scalar.copy(q_sb[:, 0, 0:P], q0_ps[0][:])
         put_q_scalar(0, 0, P)
         nc.vector.tensor_copy(q_sb[:, 1, 0:P], q0_ps[1][:])
+        put_q_vector(1, 0, 64)
 
         p_ps = [bank(f"p_ps{n}", [P, J], f"p{n}") for n in range(N // P)]
         for n in range(N // P):
@@ -235,10 +248,10 @@ def tile_list_outcomegatedpages_storeleads_kernel(
         nc.vector.tensor_copy(q_sb[:, :, P:J], q1_ps[:])
         looks0 = look(0, p_sb[0])
         looks1 = look(1, p_sb[1])
-        put_q_vector(0, P, P + 64)
-        put_q_scalar(0, P + 64, J)
-        put_q_scalar(1, 0, J)
+        put_q_scalar(0, P, J)
+        put_q_scalar(1, 64, J)
         put_m0(0, *looks0)
         put_m0(1, *looks1)
-        add_and_store(0)
-        add_and_store(1)
+        add_and_store(0, 0, E, nc.sync)
+        add_and_store(1, 0, 384, nc.sync)
+        add_and_store(1, 384, E, nc.scalar)

@@ -33,8 +33,8 @@ def tile_list_outcomegatedpages_storeleads_kernel(
         sb = ctx.enter_context(tc.tile_pool(name="sb", bufs=1))
         ps = ctx.enter_context(tc.psum_pool(name="ps", bufs=1))
 
-        def sbuf(name, shape, dtype):
-            return sb.tile(shape, dtype, name=name, align_bytes=64)
+        def sbuf(name, shape, dtype, tag=None):
+            return sb.tile(shape, dtype, name=name, tag=tag or name, align_bytes=64)
 
         def bank(name, shape, tag):
             return ps.tile(shape, F32, name=name, tag=tag)
@@ -114,12 +114,10 @@ def tile_list_outcomegatedpages_storeleads_kernel(
         identity = sbuf("identity", [P, P], F32)
         make_identity(nc, identity[:])
 
-        pw = [sbuf(f"pw{n}", [P, E], F32) for n in range(N // P)]
         pv = [sbuf(f"pv{n}", [P, E], F32) for n in range(N // P)]
-        for page in pv:
+        pw = [sbuf("pw0", [P, E], F32)]
+        for page in pv + pw:
             nc.vector.memset(page[:], 0.0)
-        for page in pw:
-            nc.gpsimd.memset(page[:], 0.0)
 
         xw = sbuf("xw", [P, J], U32)
         xs = sbuf("xs", [P, J], U8)
@@ -173,6 +171,9 @@ def tile_list_outcomegatedpages_storeleads_kernel(
         subtract(0, a0_head[:], 0, R_HEAD)
         subtract(0, a0_tail[:], R_HEAD, R)
         subtract(1, a1[:], 0, R)
+
+        pw.append(sbuf("pw1", [P, E], F32, "b_sb1"))
+        nc.vector.memset(pw[1][:], 0.0)
 
         hid_bf = []
         for jt in range(J // P):

from contextlib import ExitStack

import concourse.mybir as mybir
from concourse.masks import make_identity

K, T, J, R, V, N, U, E = 512, 1024, 256, 512, 1024, 256, 128, 512
FLOPS = 2 * K * R * J * 2 + 2 * R * N * J * 2

F32 = mybir.dt.float32
BF16 = mybir.dt.bfloat16
I32 = mybir.dt.int32
U32 = mybir.dt.uint32
U16 = mybir.dt.uint16
U8 = mybir.dt.uint8
E4M3 = mybir.dt.float8_e4m3fn_x4
E5M2 = mybir.dt.float8_e5m2_x4
E2M1 = mybir.dt.float4_e2m1fn_x4
ACT = mybir.ActivationFunctionType
ALU = mybir.AluOpType

P = 128
PACK = 4
LIST_COL = 16
R_HEAD = 384


def tile_list_outcomegatedpages_storeleads_kernel(
    tc, xt_words, xt_scales, wt_words, wt_scales, w2_words, w2_scales, wb_words, wb_scales,
    wc_words, wc_scales, so, sp, bo, offs, offs2, offs3, offs4, offs5, offs6, out,
):
    nc = tc.nc
    with ExitStack() as ctx:
        sb = ctx.enter_context(tc.tile_pool(name="sb", bufs=1))
        ps = ctx.enter_context(tc.psum_pool(name="ps", bufs=1))

        def sbuf(name, shape, dtype, tag=None):
            return sb.tile(shape, dtype, name=name, tag=tag or name, align_bytes=64)

        def bank(name, shape, tag):
            return ps.tile(shape, F32, name=name, tag=tag)

        def load_list(name, source):
            held = sbuf(name, list(source.shape), U16)
            nc.sync.dma_start(held[:], source)
            return held

        def load_words(name, source, width, dtype, queue):
            held = sbuf(name, [P, width], dtype)
            queue.dma_start(held[:].bitcast(I32), source.bitcast(I32))
            return held

        def zeroed_scales(name, width, engine):
            held = sbuf(name, [P, width], U8)
            engine.memset(held[:].bitcast(I32), 0)
            return held

        def load_scale_rows(queue, held, source, quadrants):
            for quadrant in quadrants:
                queue.dma_start(
                    held[32 * quadrant : 32 * quadrant + 32, :].bitcast(I32),
                    source[0, 4 * quadrant : 4 * quadrant + 4, :].bitcast(I32).partition_broadcast(8),
                )

        def fp8_words(source):
            return source[0].rearrange("p c r -> p (c r)")

        def load_column_pair(name, source):
            held = sbuf(name, [P, N // P], F32)
            with nc.allow_non_contiguous_dma(reason="one value a partition for each tile of n"):
                nc.sync.dma_start(held[:], source.rearrange("(t p) o -> p (t o)", p=P))
            return held

        def load_live_rows(held, source):
            for quadrant in range(4):
                nc.sync.dma_start(
                    held[32 * quadrant : 32 * quadrant + 4, :].bitcast(I32),
                    source[0, 4 * quadrant : 4 * quadrant + 4, :].bitcast(I32),
                )

        wcs = zeroed_scales("wcs", N, nc.vector)
        wbs = zeroed_scales("wbs", N, nc.vector)
        xs_all = sbuf("xs_all", [P, T], U8)
        ws_all = sbuf("ws_all", [P, V], U8)
        w2s = sbuf("w2s", [P, R], U8)

        ww_all = load_words("ww_all", wt_words[0], V, U16, nc.sync)
        load_scale_rows(nc.gpsimd, w2s, w2_scales, (2, 3))
        idx = load_list("idx", offs)
        idx2 = load_list("idx2", offs2)
        load_scale_rows(nc.sync, xs_all, xt_scales, range(4))
        xw_all = load_words("xw_all", fp8_words(xt_words), T, U32, nc.sync)

        w2w = load_words("w2w", fp8_words(w2_words), R, U32, nc.sync)
        load_scale_rows(nc.sync, w2s, w2_scales, (0, 1))
        load_scale_rows(nc.sync, ws_all, wt_scales, range(4))

        warm_in = sbuf("warm_in", [P, 1], F32)
        warm_out = sbuf("warm_out", [P, 1], F32)
        nc.vector.memset(warm_in[:], 0.0)
        nc.scalar.activation(warm_out[:], warm_in[:], ACT.Sigmoid)

        wcw = load_words("wcw", fp8_words(wc_words), N, U32, nc.sync)
        idx6 = load_list("idx6", offs6)
        idx4 = load_list("idx4", offs4)
        idx3 = load_list("idx3", offs3)
        sp_col = load_column_pair("sp_col", sp)
        bo_col = load_column_pair("bo_col", bo)
        so_col = load_column_pair("so_col", so)
        idx5 = load_list("idx5", offs5)
        wbw = load_words("wbw", wb_words[0], N, U16, nc.sync)
        load_live_rows(wcs, wc_scales)
        load_live_rows(wbs, wb_scales)

        identity = sbuf("identity", [P, P], F32)
        make_identity(nc, identity[:])

        pv = [sbuf(f"pv{n}", [P, E], F32) for n in range(N // P)]
        pw = [sbuf("pw0", [P, E], F32)]
        for page in pv + pw:
            nc.vector.memset(page[:], 0.0)

        xw = sbuf("xw", [P, J], U32)
        xs = sbuf("xs", [P, J], U8)
        ww = sbuf("ww", [P, R], U16)
        ws = sbuf("ws", [P, R], U8)

        def gather(picked, table, listed, first, last):
            nc.vector.tensor_copy(
                picked[:, first:last], table[:].indirect(listed[:, first // LIST_COL : last // LIST_COL])
            )

        def first_product(acc, jt, words, scales, dtype, first, last):
            cols = slice(jt * P, (jt + 1) * P)
            nc.tensor.matmul_mx(
                acc, lhsT=xw[:, cols].bitcast(E5M2), lhsT_scale=xs[:, cols],
                rhs=words[:, first:last].bitcast(dtype), rhs_scale=scales[:, first:last],
                start=True, stop=True,
            )

        def by_slot(ap):
            return ap.rearrange("p (m t) -> p t m", t=PACK)

        gather(ww, ww_all, idx, 0, R)
        gather(xs, xs_all, idx2, 0, J)
        gather(xw, xw_all, idx2, 0, J)

        b_sb = []
        for jt in range(J // P):
            b_ps = bank(f"b_ps{jt}", [P, R], f"turn{jt}")
            first_product(b_ps[:], jt, w2w, w2s, E4M3, 0, R)
            held = sbuf(f"b_sb{jt}", [P, PACK, R // PACK], F32)
            nc.scalar.copy(held[:], by_slot(b_ps[:]))
            b_sb.append(held)

        gather(ws, ws_all, idx, 0, R_HEAD)
        a0_head = bank("a0_head", [P, R_HEAD], "a0_head")
        first_product(a0_head[:, 0:256], 0, ww, ws, E2M1, 0, 256)
        first_product(a0_head[:, 256:R_HEAD], 0, ww, ws, E2M1, 256, R_HEAD)
        gather(ws, ws_all, idx, R_HEAD, R)
        a0_tail = bank("a0_tail", [P, R - R_HEAD], "a0_tail")
        first_product(a0_tail[:], 0, ww, ws, E2M1, R_HEAD, R)
        a1 = bank("a1", [P, R], "a1")
        first_product(a1[:], 1, ww, ws, E2M1, 0, R)

        diff = [sbuf(f"diff{jt}", [P, PACK, R // PACK], F32) for jt in range(J // P)]

        def subtract(jt, acc, first, last):
            part = slice(first // PACK, last // PACK)
            nc.vector.tensor_tensor(diff[jt][:, :, part], by_slot(acc), b_sb[jt][:, :, part], ALU.subtract)

        subtract(0, a0_head[:], 0, R_HEAD)
        subtract(0, a0_tail[:], R_HEAD, R)
        subtract(1, a1[:], 0, R)

        pw.append(sbuf("pw1", [P, E], F32, "b_sb1"))
        nc.vector.memset(pw[1][:], 0.0)

        hid_bf = []
        for jt in range(J // P):
            turned = bank(f"turned{jt}", [P, PACK, P], f"turn{jt}")
            for t in range(PACK):
                nc.tensor.transpose(turned[:, t, :], diff[jt][:, t, :], identity[:])
            held = sbuf(f"hid_bf{jt}", [P, P, PACK], BF16)
            nc.scalar.activation(held[:], turned[:].rearrange("p t j -> p j t"), ACT.Abs)
            hid_bf.append(held)

        codes = sbuf("hid_codes", [P, J], U32)
        scales = sbuf("hid_scales", [P, J], U8)
        for jt in range(J // P):
            cols = slice(jt * P, (jt + 1) * P)
            nc.vector.quantize_mx(
                codes[:, cols].bitcast(E4M3), scales[:, cols], hid_bf[jt][:].rearrange("p j t -> p (j t)")
            )

        def second_product(acc, words, wscales, dtype, n, first, last):
            cols = slice(n * P, (n + 1) * P)
            nc.tensor.matmul_mx(
                acc, lhsT=words[:, cols].bitcast(dtype), lhsT_scale=wscales[:, cols],
                rhs=codes[:, first:last].bitcast(E4M3), rhs_scale=scales[:, first:last], start=True, stop=True,
            )

        q_sb = sbuf("q_sb", [P, N // P, J], F32)

        def q_window(n, first, last):
            return pv[n][:].indirect(idx6[:, first // LIST_COL : last // LIST_COL])

        def put_q_vector(n, first, last):
            nc.vector.tensor_copy(q_window(n, first, last), q_sb[:, n, first:last])

        def put_q_scalar(n, first, last):
            nc.scalar.activation(q_window(n, first, last), q_sb[:, n, first:last], ACT.Copy)

        def look(n, p_sb):
            gate = sbuf(f"gate{n}", [P, U], F32)
            nc.scalar.activation(
                gate[:], p_sb[:].indirect(idx4[:]), ACT.Sigmoid,
                bias=bo_col[:, n : n + 1], scale=sp_col[:, n : n + 1],
            )
            weighted = sbuf(f"weighted{n}", [P, U], F32)
            nc.scalar.activation(weighted[:], p_sb[:].indirect(idx3[:]), ACT.Copy, scale=so_col[:, n : n + 1])
            return weighted, gate

        def put_m0(n, weighted, gate):
            nc.vector.tensor_tensor(pw[n][:].indirect(idx5[:]), weighted[:], gate[:], ALU.mult)

        def add_and_store(n, first, last, queue):
            result = sbuf(f"result{n}_{first}", [P, last - first], F32)
            nc.vector.tensor_tensor(result[:], pw[n][:, first:last], pv[n][:, first:last], ALU.add)
            queue.dma_start(out[n * P : (n + 1) * P, first:last], result[:])

        p_sb = [sbuf(f"p_sb{n}", [P, J], F32) for n in range(N // P)]

        q0_ps = [bank("q_ps00", [P, P], "q0"), bank("q_ps01", [P, P], "a0_tail")]
        for n in range(N // P):
            second_product(q0_ps[n][:], wcw, wcs, E4M3, n, 0, P)
        nc.scalar.copy(q_sb[:, 0, 0:P], q0_ps[0][:])
        put_q_scalar(0, 0, P)
        nc.vector.tensor_copy(q_sb[:, 1, 0:P], q0_ps[1][:])
        put_q_vector(1, 0, 64)

        p_ps = [bank(f"p_ps{n}", [P, J], f"p{n}") for n in range(N // P)]
        for n in range(N // P):
            second_product(p_ps[n][:], wbw, wbs, E2M1, n, 0, J)
        for n in range(N // P):
            nc.vector.tensor_copy(p_sb[n][:], p_ps[n][:])
        q1_ps = bank("q_ps1", [P, N // P, P], "p0")
        for n in range(N // P):
            second_product(q1_ps[:, n, :], wcw, wcs, E4M3, n, P, J)
        nc.vector.tensor_copy(q_sb[:, :, P:J], q1_ps[:])
        looks0 = look(0, p_sb[0])
        looks1 = look(1, p_sb[1])
        put_q_scalar(0, P, J)
        put_q_scalar(1, 64, J)
        put_m0(0, *looks0)
        put_m0(1, *looks1)
        add_and_store(0, 0, E, nc.sync)
        add_and_store(1, 0, 384, nc.sync)
        add_and_store(1, 384, E, nc.scalar)
